import numpy as np
import ml_dtypes


def mxq(x, axis, fmt="e4m3"):
    dtype, down = {"e4m3": (ml_dtypes.float8_e4m3fn, 7), "e5m2": (ml_dtypes.float8_e5m2, 14)}[fmt]
    v = np.moveaxis(np.asarray(x, np.float32).astype(ml_dtypes.bfloat16).astype(np.float64), axis, -1)
    blocks = v.reshape(v.shape[:-1] + (-1, 32))
    amax = np.abs(blocks).max(-1, keepdims=True)
    byte = np.maximum(np.where(amax > 0, np.frexp(amax)[1] - 1 + 127, 0) - down, 1)
    scale = np.exp2(byte - 127.0)
    codes = (blocks / scale).astype(np.float32).astype(dtype).astype(np.float64)
    return np.moveaxis((codes * scale).reshape(v.shape), -1, axis)


WIDE = False


def mx_kscale(k):
    if not WIDE:
        return np.ones(k)
    levels = np.array([10, -10, 5, -5, 0])
    if k % 512:
        return np.exp2(np.random.permutation(np.resize(levels, k // 32))).repeat(32)
    a = np.empty((k // 512, 16))
    for p in range(k // 512):
        a[p, :8] = np.random.permutation(np.resize(levels, 8))
        for g in range(8):
            far = levels[np.abs(levels - a[p, g]) >= 10]
            a[p, g + 8] = far[np.random.randint(len(far))]
    return np.exp2(a.ravel()).repeat(32)


def f64(x):
    return np.asarray(x).astype(np.float64)


def striped(idx):
    return np.tile(idx.reshape(-1, 16).T, (8, 1)).astype(np.uint16)


def unstriped(offs):
    return offs[:16].T.reshape(-1).astype(np.int64)


E2M1 = np.array([0.0, 0.5, 1.0, 1.5, 2.0, 3.0, 4.0, 6.0, -0.0, -0.5, -1.0, -1.5, -2.0, -3.0, -4.0, -6.0])


def pack_weight(w, fmt):
    k, n = w.shape
    w = f64(np.asarray(w, np.float32).astype(ml_dtypes.bfloat16)).reshape(k // 32, 32, n)
    amax = np.abs(w).max(1)
    if fmt == "e4m3":
        byte = np.frexp(amax)[1] - 1 + 127 - 7
    else:
        mant, ex = np.frexp(amax / 6.0)
        byte = np.where(mant > 0.5, ex, ex - 1) + 127
    byte = np.clip(np.where(amax > 0, byte, 1), 1, 254)
    scaled = (w * np.exp2(127.0 - byte)[:, None, :]).reshape(k, n).astype(np.float32)
    by_word = np.ascontiguousarray(scaled.reshape(k // 512, 128, 4, n).transpose(0, 1, 3, 2))
    if fmt == "e4m3":
        words = by_word.astype(ml_dtypes.float8_e4m3fn).view(np.uint8)
    else:
        c = by_word.astype(ml_dtypes.float4_e2m1fn).view(np.uint8) & 0xF
        words = (c[..., 0::2] | (c[..., 1::2] << 4)).reshape(k // 512, 128, 2 * n)
    return np.ascontiguousarray(words), np.ascontiguousarray(byte.astype(np.uint8).reshape(k // 512, 16, n))


def unpack_weight(words, scales, fmt):
    g, _, n = scales.shape
    words = np.ascontiguousarray(words).reshape(g, 128, n, -1)
    if fmt == "e4m3":
        vals = words.view(ml_dtypes.float8_e4m3fn).astype(np.float64)
    else:
        nib = np.empty((g, 128, n, 4), np.uint8)
        nib[..., 0::2] = words & 0xF
        nib[..., 1::2] = words >> 4
        vals = E2M1[nib]
    vals = vals * np.repeat(np.exp2(scales.astype(np.float64) - 127.0), 8, axis=1)[..., None]
    return vals.transpose(0, 1, 3, 2).reshape(g * 512, n)


def gelu(v):
    return 0.5 * v * (1.0 + np.tanh(np.sqrt(2.0 / np.pi) * (v + 0.044715 * v**3)))


K, T, E, C, H, N = 2048, 768, 2, 256, 512, 256


def by_expert(wq, xq):
    return np.concatenate([wq[e].T @ xq[:, e * C:(e + 1) * C] for e in range(E)], axis=1)


def setup_inputs():
    n = np.random.standard_normal
    s = mx_kscale(K)[:, None]
    u = mx_kscale(H)
    w1 = [pack_weight(m, "e2m1") for m in n((E, K, H)) / np.sqrt(K) / s[None] * u[None, None, :]]
    w2 = [pack_weight(m, "e2m1") for m in n((E, H, N)) / np.sqrt(H) / u[None, :, None]]
    return {
        "xT": (n((K, T)) * s).astype(np.float32),
        "xr": n((N, T)).astype(np.float32),
        "w1_words": np.stack([m[0] for m in w1]),
        "w1_scales": np.stack([m[1] for m in w1]),
        "w2_words": np.stack([m[0] for m in w2]),
        "w2_scales": np.stack([m[1] for m in w2]),
        "gate": np.tile(np.random.uniform(0.2, 1.0, E * C), (N, 1)).astype(np.float32),
        "offs": striped(np.random.permutation(T)[:E * C]),
    }


def reference(xT, xr, w1_words, w1_scales, w2_words, w2_scales, gate, offs):
    idx = unstriped(offs)
    w1 = np.stack([unpack_weight(w1_words[e], w1_scales[e], "e2m1") for e in range(E)])
    w2 = np.stack([unpack_weight(w2_words[e], w2_scales[e], "e2m1") for e in range(E)])
    xq = mxq(f64(xT)[:, idx], 0, "e4m3")
    h = gelu(by_expert(w1, xq))
    y = by_expert(w2, mxq(h, 0, "e4m3"))
    out = f64(xr).copy()
    out[:, idx] += f64(gate) * y
    return out

@@ -1,0 +1,205 @@
+from contextlib import ExitStack
+
+import concourse.mybir as mybir
+from concourse.masks import make_identity
+
+K, T, E, C, H, N = 2048, 768, 2, 256, 512, 256
+P = 128
+S = K // 512
+SLOTS = E * C
+A = 512
+
+FLOPS = 2 * SLOTS * H * (K + N)
+BYTES = K * T * 4 + 2 * N * T * 4 + E * K * H // 2 + E * K * H // 32 + E * H * N // 2 + E * H * N // 32 + SLOTS * 4 + SLOTS * 2
+
+F32 = mybir.dt.float32
+BF16 = mybir.dt.bfloat16
+I32 = mybir.dt.int32
+U32 = mybir.dt.uint32
+U16 = mybir.dt.uint16
+U8 = mybir.dt.uint8
+FP8X4 = mybir.dt.float8_e4m3fn_x4
+FP4X4 = mybir.dt.float4_e2m1fn_x4
+ACT = mybir.ActivationFunctionType
+MULT = mybir.AluOpType.mult
+ADD = mybir.AluOpType.add
+
+
+def tile_moe_res_mlp_gelu_kernel(tc, xT, xr, w1_words, w1_scales, w2_words, w2_scales, gate, offs, out):
+    nc = tc.nc
+    with ExitStack() as ctx:
+        held = ctx.enter_context(tc.tile_pool(name="held", bufs=1))
+        psum = ctx.enter_context(tc.psum_pool(name="psum", bufs=1))
+
+        offsets = held.tile([P, SLOTS // 16], U16, name="offsets")
+        x = [held.tile([P, 4, T], F32, name=f"x{s}") for s in range(S)]
+        xb = [held.tile([P, T, 4], BF16, name=f"xb{s}", align_bytes=64) for s in range(S)]
+        xw = [held.tile([P, T], U32, name=f"xw{s}", align_bytes=64) for s in range(S)]
+        xs = [held.tile([P, T], U8, name=f"xs{s}", align_bytes=64) for s in range(2)]
+        gw = [held.tile([P, SLOTS], U32, name=f"gw{s}", align_bytes=64) for s in range(S)]
+        gs = [held.tile([P, SLOTS], U8, name=f"gs{s}", align_bytes=64) for s in range(S)]
+        w1 = [held.tile([P, S, 2 * H], U8, name=f"w1_{e}", align_bytes=64) for e in range(E)]
+        w1s = held.tile([P, E * S, H], U8, name="w1s", align_bytes=64)
+        w2 = held.tile([P, E, 2 * N], U8, name="w2", align_bytes=64)
+        w2s = held.tile([P, E, N], U8, name="w2s", align_bytes=64)
+        g = held.tile([P, SLOTS], F32, name="g")
+        res = [held.tile([P, T], F32, name=f"res{n}") for n in range(2)]
+        win = [held.tile([P, T], F32, name=f"win{n}") for n in range(2)]
+        o = [held.tile([P, T], F32, name=f"o{n}") for n in range(2)]
+        h = [held.tile([P, H], BF16, name=f"h{m}", align_bytes=64) for m in range(4)]
+        hg = [held.tile([P, C * 4], BF16, name=f"hg{e}", align_bytes=64) for e in range(E)]
+        hw = [held.tile([P, C], U32, name=f"hw{e}", align_bytes=64) for e in range(E)]
+        hs = [held.tile([P, C], U8, name=f"hs{e}", align_bytes=64) for e in range(E)]
+        y = [held.tile([P, 2, C], F32, name=f"y{e}") for e in range(E)]
+        ident = held.tile([P, P], F32, name="ident")
+        warm = held.tile([P, 1], F32, name="warm")
+
+        pa = [psum.tile([P, H], F32, name=f"pa{m}") for m in range(4)]
+        pt = [psum.tile([P, 2, 2, P], F32, name=f"pt{e}") for e in range(E)]
+        py = [psum.tile([P, 2, C], F32, name=f"py{e}") for e in range(E)]
+
+        nc.vector.memset(w1s[:].rearrange("p a b -> p (a b)").bitcast(I32), 0)
+        nc.vector.memset(w2s[:].rearrange("p a b -> p (a b)").bitcast(I32), 0)
+        nc.vector.memset(warm[:], 0.0)
+        for s in range(2):
+            nc.vector.memset(xs[s][:].bitcast(I32), 0)
+        for s in (1, 2):
+            nc.gpsimd.memset(gs[s][:].bitcast(I32), 0)
+        make_identity(nc, ident[:])
+        for n in range(2):
+            nc.gpsimd.memset(win[n][:], 0.0)
+
+        def load_x(s, a, b):
+            nc.sync.dma_start(x[s][:, :, a:b], xT[512 * s : 512 * s + 512, a:b].rearrange("(p j) t -> p j t", j=4))
+
+        def load_w1(e):
+            nc.sync.dma_start(w1[e][:].bitcast(I32), w1_words[e].rearrange("s p b -> p s b").bitcast(I32))
+
+        for b in range(0, T, C):
+            load_x(0, b, b + C)
+        nc.sync.dma_start(offsets[:], offs)
+        for quad in range(4):
+            nc.scalar.dma_start(
+                w1s[32 * quad : 32 * quad + 4].bitcast(I32),
+                w1_scales.rearrange("e s q i -> q (e s) i")[4 * quad : 4 * quad + 4].bitcast(I32),
+            )
+        nc.scalar.activation(warm[:], warm[:], ACT.Gelu_apprx_tanh)
+        load_x(1, 0, T)
+        load_x(2, 0, T)
+        load_x(3, 0, A)
+        load_x(3, A, T)
+        load_w1(0)
+        load_w1(1)
+        nc.sync.dma_start(w2[:].bitcast(I32), w2_words.rearrange("e s p b -> p (e s) b").bitcast(I32))
+        for quad in range(4):
+            nc.gpsimd.dma_start(
+                w2s[32 * quad : 32 * quad + 4].bitcast(I32),
+                w2_scales.rearrange("e s q i -> q (e s) i")[4 * quad : 4 * quad + 4].bitcast(I32),
+            )
+
+        def cast(engine, s, a, b):
+            dst = xb[s][:, a:b, :].rearrange("p (c i) j -> p c j i", i=4)
+            src = x[s][:, :, a:b].rearrange("p j (c i) -> p c j i", i=4)
+            if engine == "s":
+                nc.scalar.activation(dst, src, ACT.Copy)
+            else:
+                nc.vector.tensor_copy(dst, src)
+
+        def quant(s, a, b):
+            scales = xs[1][:, a:b] if s == S - 1 else xs[0][4 * s : P, a:b]
+            nc.vector.quantize_mx(
+                out=xw[s][:, a:b].bitcast(FP8X4),
+                scales=scales,
+                in_=xb[s][:, a:b, :].rearrange("p t j -> p (t j)"),
+            )
+
+        def gather_words(s, e0, e1):
+            nc.vector.tensor_copy(gw[s][:, e0 * C : e1 * C], xw[s][:].indirect(offsets[:, e0 * C // 16 : e1 * C // 16]))
+
+        def gather_scales(s, e0, e1):
+            nc.vector.tensor_copy(gs[s][:, e0 * C : e1 * C], xs[s // 3][:].indirect(offsets[:, e0 * C // 16 : e1 * C // 16]))
+
+        def up(s, m):
+            e = m // 2
+            cols = slice(P * m, P * m + P)
+            nc.tensor.matmul_mx(
+                out=pa[m][:],
+                lhsT=gw[s][:, cols].bitcast(FP8X4),
+                lhsT_scale=gs[s][:, cols],
+                rhs=w1[e][:, s, :].bitcast(FP4X4),
+                rhs_scale=w1s[:, e * S + s, :],
+                start=(s == 0),
+                stop=(s == S - 1),
+            )
+
+        last = S - 1
+        for b in range(0, T, C):
+            cast("s", 0, b, b + 128)
+            cast("v", 0, b + 128, b + C)
+            quant(0, b, b + C)
+        gather_words(0, 0, E)
+        cast("s", 1, 0, 256)
+        cast("v", 1, 256, T)
+        quant(1, A, T)
+        quant(1, 0, A)
+        gather_words(1, 0, 1)
+        cast("s", 2, 0, 320)
+        cast("v", 2, 320, T)
+        quant(2, A, T)
+        quant(2, 0, A)
+        gather_scales(0, 0, E)
+        for s in (1, 2):
+            nc.sync.dma_start(gs[s][0 : P - 4 * s, :].bitcast(I32), gs[0][4 * s : P, :].bitcast(I32))
+        nc.sync.dma_start(g[:], gate[0:P, :])
+        for n in range(2):
+            nc.sync.dma_start(res[n][:], xr[P * n : P * n + P, :])
+        gather_words(2, 0, 1)
+        cast("s", last, 0, 320)
+        cast("v", last, 320, A)
+        cast("s", last, A, 704)
+        cast("v", last, 704, T)
+        quant(last, 0, A)
+        quant(last, A, T)
+
+        for e in range(E):
+            if e == 1:
+                gather_words(1, 1, 2)
+                gather_words(2, 1, 2)
+            gather_scales(last, e, e + 1)
+            gather_words(last, e, e + 1)
+            for s in range(last):
+                for m in (2 * e, 2 * e + 1):
+                    up(s, m)
+            for i in range(2):
+                m = 2 * e + i
+                up(last, m)
+                nc.scalar.activation(h[m][:], pa[m][:], ACT.Gelu_apprx_tanh)
+                words = h[m][:].bitcast(F32)
+                for u in range(2):
+                    nc.tensor.transpose(pt[e][:, i, u, :], words[:, u : H // 2 : 2], ident[:])
+                copy = nc.vector.tensor_copy if e == 0 else nc.scalar.copy
+                copy(
+                    hg[e][:, H * i : H * i + H].bitcast(F32).rearrange("p (r u) -> p r u", u=2),
+                    pt[e][:, i].rearrange("p u r -> p r u"),
+                )
+            nc.vector.quantize_mx(out=hw[e][:].bitcast(FP8X4), scales=hs[e][:], in_=hg[e][:])
+            for n in range(2):
+                nc.tensor.matmul_mx(
+                    out=py[e][:, n, :],
+                    lhsT=w2[:, e, N * n : N * n + N].bitcast(FP4X4),
+                    lhsT_scale=w2s[:, e, P * n : P * n + P],
+                    rhs=hw[e][:].bitcast(FP8X4),
+                    rhs_scale=hs[e][:],
+                    start=True,
+                    stop=True,
+                )
+        for e in range(E):
+            lst = offsets[:, e * C // 16 : (e + 1) * C // 16]
+            for n in range(2):
+                nc.vector.tensor_tensor(y[e][:, n, :], py[e][:, n, :], g[:, e * C : (e + 1) * C], MULT)
+                nc.vector.tensor_copy(win[n][:].indirect(lst), y[e][:, n, :])
+        for n in range(2):
+            for a, b in ((0, T // 2), (T // 2, T)):
+                engine = nc.gpsimd if n == 0 else nc.vector
+                engine.tensor_tensor(o[n][:, a:b], win[n][:, a:b], res[n][:, a:b], ADD)
+                nc.sync.dma_start(out[P * n : P * n + P, a:b], o[n][:, a:b])

@@ -78,16 +78,16 @@ def tile_moe_res_mlp_gelu_kernel(tc, xT, xr, w1_words, w1_scales, w2_words, w2_s
         for b in range(0, T, C):
             load_x(0, b, b + C)
         nc.sync.dma_start(offsets[:], offs)
-        for quad in range(4):
-            nc.scalar.dma_start(
-                w1s[32 * quad : 32 * quad + 4].bitcast(I32),
-                w1_scales.rearrange("e s q i -> q (e s) i")[4 * quad : 4 * quad + 4].bitcast(I32),
-            )
         nc.scalar.activation(warm[:], warm[:], ACT.Gelu_apprx_tanh)
         load_x(1, 0, T)
         load_x(2, 0, T)
         load_x(3, 0, A)
         load_x(3, A, T)
+        for quad in range(4):
+            nc.sync.dma_start(
+                w1s[32 * quad : 32 * quad + 4].bitcast(I32),
+                w1_scales.rearrange("e s q i -> q (e s) i")[4 * quad : 4 * quad + 4].bitcast(I32),
+            )
         load_w1(0)
         load_w1(1)
         nc.sync.dma_start(w2[:].bitcast(I32), w2_words.rearrange("e s p b -> p (e s) b").bitcast(I32))
@@ -137,34 +137,34 @@ def tile_moe_res_mlp_gelu_kernel(tc, xT, xr, w1_words, w1_scales, w2_words, w2_s
             cast("s", 0, b, b + 128)
             cast("v", 0, b + 128, b + C)
             quant(0, b, b + C)
-        gather_words(0, 0, E)
-        cast("s", 1, 0, 256)
-        cast("v", 1, 256, T)
+        cast("s", 1, 0, 384)
+        cast("v", 1, 384, T)
+        gather_words(0, 0, 1)
         quant(1, A, T)
         quant(1, 0, A)
+        gather_words(0, 1, 2)
+        cast("s", 2, 0, A)
+        cast("v", 2, A, T)
         gather_words(1, 0, 1)
-        cast("s", 2, 0, 320)
-        cast("v", 2, 320, T)
         quant(2, A, T)
         quant(2, 0, A)
+        gather_words(1, 1, 2)
         gather_scales(0, 0, E)
         for s in (1, 2):
             nc.sync.dma_start(gs[s][0 : P - 4 * s, :].bitcast(I32), gs[0][4 * s : P, :].bitcast(I32))
         nc.sync.dma_start(g[:], gate[0:P, :])
         for n in range(2):
             nc.sync.dma_start(res[n][:], xr[P * n : P * n + P, :])
-        gather_words(2, 0, 1)
-        cast("s", last, 0, 320)
-        cast("v", last, 320, A)
+        cast("s", last, 0, 384)
+        cast("v", last, 384, A)
         cast("s", last, A, 704)
         cast("v", last, 704, T)
+        gather_words(2, 0, 1)
         quant(last, 0, A)
         quant(last, A, T)
+        gather_words(2, 1, 2)
 
         for e in range(E):
-            if e == 1:
-                gather_words(1, 1, 2)
-                gather_words(2, 1, 2)
             gather_scales(last, e, e + 1)
             gather_words(last, e, e + 1)
             for s in range(last):
@@ -182,7 +182,9 @@ def tile_moe_res_mlp_gelu_kernel(tc, xT, xr, w1_words, w1_scales, w2_words, w2_s
                     hg[e][:, H * i : H * i + H].bitcast(F32).rearrange("p (r u) -> p r u", u=2),
                     pt[e][:, i].rearrange("p u r -> p r u"),
                 )
-            nc.vector.quantize_mx(out=hw[e][:].bitcast(FP8X4), scales=hs[e][:], in_=hg[e][:])
+            for i in range(2):
+                cols = slice(P * i, P * i + P)
+                nc.vector.quantize_mx(out=hw[e][:, cols].bitcast(FP8X4), scales=hs[e][:, cols], in_=hg[e][:, H * i : H * i + H])
             for n in range(2):
                 nc.tensor.matmul_mx(
                     out=py[e][:, n, :],
@@ -197,6 +199,7 @@ def tile_moe_res_mlp_gelu_kernel(tc, xT, xr, w1_words, w1_scales, w2_words, w2_s
             lst = offsets[:, e * C // 16 : (e + 1) * C // 16]
             for n in range(2):
                 nc.vector.tensor_tensor(y[e][:, n, :], py[e][:, n, :], g[:, e * C : (e + 1) * C], MULT)
+            for n in range(2):
                 nc.vector.tensor_copy(win[n][:].indirect(lst), y[e][:, n, :])
         for n in range(2):
             for a, b in ((0, T // 2), (T // 2, T)):

@@ -35,10 +35,10 @@ def tile_moe_res_mlp_gelu_kernel(tc, xT, xr, w1_words, w1_scales, w2_words, w2_s
         x = [held.tile([P, 4, T], F32, name=f"x{s}") for s in range(S)]
         xb = [held.tile([P, T, 4], BF16, name=f"xb{s}", align_bytes=64) for s in range(S)]
         xw = [held.tile([P, T], U32, name=f"xw{s}", align_bytes=64) for s in range(S)]
-        xs = [held.tile([P, T], U8, name=f"xs{s}", align_bytes=64) for s in range(2)]
+        xs = [held.tile([P, T], U8, name=f"xs{s}", align_bytes=64) for s in range(S)]
         gw = [held.tile([P, SLOTS], U32, name=f"gw{s}", align_bytes=64) for s in range(S)]
         gs = [held.tile([P, SLOTS], U8, name=f"gs{s}", align_bytes=64) for s in range(S)]
-        w1 = [held.tile([P, S, 2 * H], U8, name=f"w1_{e}", align_bytes=64) for e in range(E)]
+        w1 = held.tile([P, E, S, 2 * H], U8, name="w1", align_bytes=64)
         w1s = held.tile([P, E * S, H], U8, name="w1s", align_bytes=64)
         w2 = held.tile([P, E, 2 * N], U8, name="w2", align_bytes=64)
         w2s = held.tile([P, E, N], U8, name="w2s", align_bytes=64)
@@ -61,10 +61,8 @@ def tile_moe_res_mlp_gelu_kernel(tc, xT, xr, w1_words, w1_scales, w2_words, w2_s
         nc.vector.memset(w1s[:].rearrange("p a b -> p (a b)").bitcast(I32), 0)
         nc.vector.memset(w2s[:].rearrange("p a b -> p (a b)").bitcast(I32), 0)
         nc.vector.memset(warm[:], 0.0)
-        for s in range(2):
+        for s in range(S):
             nc.vector.memset(xs[s][:].bitcast(I32), 0)
-        for s in (1, 2):
-            nc.gpsimd.memset(gs[s][:].bitcast(I32), 0)
         make_identity(nc, ident[:])
         for n in range(2):
             nc.gpsimd.memset(win[n][:], 0.0)
@@ -72,24 +70,33 @@ def tile_moe_res_mlp_gelu_kernel(tc, xT, xr, w1_words, w1_scales, w2_words, w2_s
         def load_x(s, a, b):
             nc.sync.dma_start(x[s][:, :, a:b], xT[512 * s : 512 * s + 512, a:b].rearrange("(p j) t -> p j t", j=4))
 
-        def load_w1(e):
-            nc.sync.dma_start(w1[e][:].bitcast(I32), w1_words[e].rearrange("s p b -> p s b").bitcast(I32))
+        def load_w1(e0, e1, s0, s1):
+            for e in range(e0, e1):
+                nc.sync.dma_start(w1[:, e, s0:s1, :].bitcast(I32), w1_words[e, s0:s1].rearrange("s p b -> p s b").bitcast(I32))
+
+        def load_w1s(e):
+            for quad in range(4):
+                nc.sync.dma_start(
+                    w1s[32 * quad : 32 * quad + 4, e * S : e * S + S, :].bitcast(I32),
+                    w1_scales[e, :, 4 * quad : 4 * quad + 4, :].rearrange("s q i -> q s i").bitcast(I32),
+                )
 
         for b in range(0, T, C):
             load_x(0, b, b + C)
         nc.sync.dma_start(offsets[:], offs)
         nc.scalar.activation(warm[:], warm[:], ACT.Gelu_apprx_tanh)
-        load_x(1, 0, T)
-        load_x(2, 0, T)
+        load_x(1, 0, A)
+        load_x(1, A, T)
+        load_x(2, 0, A)
+        load_x(2, A, T)
+        load_w1(0, 1, 0, 2)
         load_x(3, 0, A)
         load_x(3, A, T)
-        for quad in range(4):
-            nc.sync.dma_start(
-                w1s[32 * quad : 32 * quad + 4].bitcast(I32),
-                w1_scales.rearrange("e s q i -> q (e s) i")[4 * quad : 4 * quad + 4].bitcast(I32),
-            )
-        load_w1(0)
-        load_w1(1)
+        load_w1s(0)
+        load_w1(1, 2, 0, 2)
+        load_w1(0, 1, 2, 4)
+        load_w1s(1)
+        load_w1(1, 2, 2, 4)
         nc.sync.dma_start(w2[:].bitcast(I32), w2_words.rearrange("e s p b -> p (e s) b").bitcast(I32))
         for quad in range(4):
             nc.gpsimd.dma_start(
@@ -98,18 +105,17 @@ def tile_moe_res_mlp_gelu_kernel(tc, xT, xr, w1_words, w1_scales, w2_words, w2_s
             )
 
         def cast(engine, s, a, b):
-            dst = xb[s][:, a:b, :].rearrange("p (c i) j -> p c j i", i=4)
-            src = x[s][:, :, a:b].rearrange("p j (c i) -> p c j i", i=4)
+            dst = xb[s][:, a:b, :]
+            src = x[s][:, :, a:b].rearrange("p j t -> p t j")
             if engine == "s":
                 nc.scalar.activation(dst, src, ACT.Copy)
             else:
                 nc.vector.tensor_copy(dst, src)
 
         def quant(s, a, b):
-            scales = xs[1][:, a:b] if s == S - 1 else xs[0][4 * s : P, a:b]
             nc.vector.quantize_mx(
                 out=xw[s][:, a:b].bitcast(FP8X4),
-                scales=scales,
+                scales=xs[s][:, a:b],
                 in_=xb[s][:, a:b, :].rearrange("p t j -> p (t j)"),
             )
 
@@ -117,7 +123,7 @@ def tile_moe_res_mlp_gelu_kernel(tc, xT, xr, w1_words, w1_scales, w2_words, w2_s
             nc.vector.tensor_copy(gw[s][:, e0 * C : e1 * C], xw[s][:].indirect(offsets[:, e0 * C // 16 : e1 * C // 16]))
 
         def gather_scales(s, e0, e1):
-            nc.vector.tensor_copy(gs[s][:, e0 * C : e1 * C], xs[s // 3][:].indirect(offsets[:, e0 * C // 16 : e1 * C // 16]))
+            nc.vector.tensor_copy(gs[s][:, e0 * C : e1 * C], xs[s][:].indirect(offsets[:, e0 * C // 16 : e1 * C // 16]))
 
         def up(s, m):
             e = m // 2
@@ -126,65 +132,71 @@ def tile_moe_res_mlp_gelu_kernel(tc, xT, xr, w1_words, w1_scales, w2_words, w2_s
                 out=pa[m][:],
                 lhsT=gw[s][:, cols].bitcast(FP8X4),
                 lhsT_scale=gs[s][:, cols],
-                rhs=w1[e][:, s, :].bitcast(FP4X4),
+                rhs=w1[:, e, s, :].bitcast(FP4X4),
                 rhs_scale=w1s[:, e * S + s, :],
                 start=(s == 0),
                 stop=(s == S - 1),
             )
 
-        last = S - 1
-        for b in range(0, T, C):
-            cast("s", 0, b, b + 128)
-            cast("v", 0, b + 128, b + C)
-            quant(0, b, b + C)
-        cast("s", 1, 0, 384)
-        cast("v", 1, 384, T)
-        gather_words(0, 0, 1)
-        quant(1, A, T)
-        quant(1, 0, A)
-        gather_words(0, 1, 2)
-        cast("s", 2, 0, A)
-        cast("v", 2, A, T)
-        gather_words(1, 0, 1)
-        quant(2, A, T)
-        quant(2, 0, A)
-        gather_words(1, 1, 2)
-        gather_scales(0, 0, E)
-        for s in (1, 2):
-            nc.sync.dma_start(gs[s][0 : P - 4 * s, :].bitcast(I32), gs[0][4 * s : P, :].bitcast(I32))
         nc.sync.dma_start(g[:], gate[0:P, :])
         for n in range(2):
             nc.sync.dma_start(res[n][:], xr[P * n : P * n + P, :])
-        cast("s", last, 0, 384)
-        cast("v", last, 384, A)
-        cast("s", last, A, 704)
-        cast("v", last, 704, T)
-        gather_words(2, 0, 1)
-        quant(last, 0, A)
-        quant(last, A, T)
-        gather_words(2, 1, 2)
 
-        for e in range(E):
-            gather_scales(last, e, e + 1)
-            gather_words(last, e, e + 1)
-            for s in range(last):
-                for m in (2 * e, 2 * e + 1):
-                    up(s, m)
-            for i in range(2):
-                m = 2 * e + i
-                up(last, m)
-                nc.scalar.activation(h[m][:], pa[m][:], ACT.Gelu_apprx_tanh)
-                words = h[m][:].bitcast(F32)
-                for u in range(2):
-                    nc.tensor.transpose(pt[e][:, i, u, :], words[:, u : H // 2 : 2], ident[:])
-                copy = nc.vector.tensor_copy if e == 0 else nc.scalar.copy
-                copy(
-                    hg[e][:, H * i : H * i + H].bitcast(F32).rearrange("p (r u) -> p r u", u=2),
-                    pt[e][:, i].rearrange("p u r -> p r u"),
-                )
-            for i in range(2):
-                cols = slice(P * i, P * i + P)
-                nc.vector.quantize_mx(out=hw[e][:, cols].bitcast(FP8X4), scales=hs[e][:, cols], in_=hg[e][:, H * i : H * i + H])
+        last = S - 1
+        cast("s", 0, 0, 192)
+        cast("v", 0, 192, 256)
+        quant(0, 0, 256)
+        cast("s", 0, 256, 448)
+        cast("v", 0, 448, 512)
+        quant(0, 256, 512)
+        cast("s", 0, 512, 704)
+        cast("v", 0, 704, 768)
+        quant(0, 512, 768)
+        gather_scales(0, 0, E)
+        cast("s", 1, 0, 288)
+        cast("v", 1, 288, 512)
+        cast("s", 1, 512, 544)
+        cast("v", 1, 544, 768)
+        gather_words(0, 0, 1)
+        quant(1, 0, A)
+        quant(1, A, T)
+        gather_words(0, 1, 2)
+        cast("s", 2, 0, 448)
+        cast("v", 2, 448, 512)
+        cast("s", 2, 512, 736)
+        cast("v", 2, 736, 768)
+        gather_scales(1, 0, E)
+        gather_words(1, 0, 1)
+        quant(2, 0, A)
+        quant(2, A, T)
+        gather_words(1, 1, 2)
+        cast("s", 3, 0, 480)
+        cast("v", 3, 480, 512)
+        gather_scales(2, 0, E)
+        cast("s", 3, 512, 672)
+        cast("v", 3, 672, 768)
+        gather_words(2, 0, 1)
+        quant(3, 0, A)
+        quant(3, A, T)
+
+        def gelu_turn(m):
+            nc.scalar.activation(h[m][:], pa[m][:], ACT.Gelu_apprx_tanh)
+            words = h[m][:].bitcast(F32)
+            for u in range(2):
+                nc.tensor.transpose(pt[m // 2][:, m % 2, u, :], words[:, u : H // 2 : 2], ident[:])
+
+        def lay(m, copy):
+            i = m % 2
+            copy(
+                hg[m // 2][:, H * i : H * i + H].bitcast(F32).rearrange("p (r u) -> p r u", u=2),
+                pt[m // 2][:, i].rearrange("p u r -> p r u"),
+            )
+
+        def quant_h(m):
+            e, cols = m // 2, slice(P * (m % 2), P * (m % 2) + P)
+            nc.vector.quantize_mx(out=hw[e][:, cols].bitcast(FP8X4), scales=hs[e][:, cols], in_=hg[e][:, H * (m % 2) : H * (m % 2) + H])
+
+        def down(e):
             for n in range(2):
                 nc.tensor.matmul_mx(
                     out=py[e][:, n, :],
@@ -195,12 +207,56 @@ def tile_moe_res_mlp_gelu_kernel(tc, xT, xr, w1_words, w1_scales, w2_words, w2_s
                     start=True,
                     stop=True,
                 )
-        for e in range(E):
-            lst = offsets[:, e * C // 16 : (e + 1) * C // 16]
-            for n in range(2):
-                nc.vector.tensor_tensor(y[e][:, n, :], py[e][:, n, :], g[:, e * C : (e + 1) * C], MULT)
-            for n in range(2):
-                nc.vector.tensor_copy(win[n][:].indirect(lst), y[e][:, n, :])
+
+        def weigh(e, n):
+            nc.vector.tensor_tensor(y[e][:, n, :], py[e][:, n, :], g[:, e * C : (e + 1) * C], MULT)
+
+        def scatter(e, n):
+            nc.vector.tensor_copy(win[n][:].indirect(offsets[:, e * C // 16 : (e + 1) * C // 16]), y[e][:, n, :])
+
+        up(0, 0)
+        up(1, 0)
+        up(2, 0)
+        up(0, 1)
+        up(1, 1)
+        up(2, 1)
+        gather_scales(3, 0, 1)
+        gather_words(3, 0, 1)
+        up(3, 0)
+        up(3, 1)
+        gelu_turn(0)
+        gelu_turn(1)
+        gather_words(2, 1, 2)
+        gather_scales(3, 1, 2)
+        gather_words(3, 1, 2)
+        lay(0, nc.scalar.copy)
+        lay(1, nc.vector.tensor_copy)
+        quant_h(0)
+        quant_h(1)
+        down(0)
+        up(0, 2)
+        up(1, 2)
+        up(2, 2)
+        up(0, 3)
+        up(1, 3)
+        up(2, 3)
+        up(3, 2)
+        up(3, 3)
+        gelu_turn(2)
+        gelu_turn(3)
+        lay(2, nc.scalar.copy)
+        lay(3, nc.scalar.copy)
+        weigh(0, 0)
+        weigh(0, 1)
+        scatter(0, 0)
+        quant_h(2)
+        quant_h(3)
+        down(1)
+        scatter(0, 1)
+        weigh(1, 0)
+        weigh(1, 1)
+        scatter(1, 0)
+        scatter(1, 1)
         for n in range(2):
             for a, b in ((0, T // 2), (T // 2, T)):
                 engine = nc.gpsimd if n == 0 else nc.vector

from contextlib import ExitStack

import concourse.mybir as mybir
from concourse.masks import make_identity

K, T, E, C, H, N = 2048, 768, 2, 256, 512, 256
P = 128
S = K // 512
SLOTS = E * C
A = 512

FLOPS = 2 * SLOTS * H * (K + N)
BYTES = K * T * 4 + 2 * N * T * 4 + E * K * H // 2 + E * K * H // 32 + E * H * N // 2 + E * H * N // 32 + SLOTS * 4 + SLOTS * 2

F32 = mybir.dt.float32
BF16 = mybir.dt.bfloat16
I32 = mybir.dt.int32
U32 = mybir.dt.uint32
U16 = mybir.dt.uint16
U8 = mybir.dt.uint8
FP8X4 = mybir.dt.float8_e4m3fn_x4
FP4X4 = mybir.dt.float4_e2m1fn_x4
ACT = mybir.ActivationFunctionType
MULT = mybir.AluOpType.mult
ADD = mybir.AluOpType.add


def tile_moe_res_mlp_gelu_kernel(tc, xT, xr, w1_words, w1_scales, w2_words, w2_scales, gate, offs, out):
    nc = tc.nc
    with ExitStack() as ctx:
        held = ctx.enter_context(tc.tile_pool(name="held", bufs=1))
        psum = ctx.enter_context(tc.psum_pool(name="psum", bufs=1))

        offsets = held.tile([P, SLOTS // 16], U16, name="offsets")
        x = [held.tile([P, 4, T], F32, name=f"x{s}") for s in range(S)]
        xb = [held.tile([P, T, 4], BF16, name=f"xb{s}", align_bytes=64) for s in range(S)]
        xw = [held.tile([P, T], U32, name=f"xw{s}", align_bytes=64) for s in range(S)]
        xs = [held.tile([P, T], U8, name=f"xs{s}", align_bytes=64) for s in range(S)]
        gw = [held.tile([P, SLOTS], U32, name=f"gw{s}", align_bytes=64) for s in range(S)]
        gs = [held.tile([P, SLOTS], U8, name=f"gs{s}", align_bytes=64) for s in range(S)]
        w1 = held.tile([P, E, S, 2 * H], U8, name="w1", align_bytes=64)
        w1s = held.tile([P, E * S, H], U8, name="w1s", align_bytes=64)
        w2 = held.tile([P, E, 2 * N], U8, name="w2", align_bytes=64)
        w2s = held.tile([P, E, N], U8, name="w2s", align_bytes=64)
        g = held.tile([P, SLOTS], F32, name="g")
        res = [held.tile([P, T], F32, name=f"res{n}") for n in range(2)]
        win = [held.tile([P, T], F32, name=f"win{n}") for n in range(2)]
        o = [held.tile([P, T], F32, name=f"o{n}") for n in range(2)]
        h = [held.tile([P, H], BF16, name=f"h{m}", align_bytes=64) for m in range(4)]
        hg = [held.tile([P, C * 4], BF16, name=f"hg{e}", align_bytes=64) for e in range(E)]
        hw = [held.tile([P, C], U32, name=f"hw{e}", align_bytes=64) for e in range(E)]
        hs = [held.tile([P, C], U8, name=f"hs{e}", align_bytes=64) for e in range(E)]
        y = [held.tile([P, 2, C], F32, name=f"y{e}") for e in range(E)]
        ident = held.tile([P, P], F32, name="ident")
        warm = held.tile([P, 1], F32, name="warm")

        pa = [psum.tile([P, H], F32, name=f"pa{m}") for m in range(4)]
        pt = [psum.tile([P, 2, 2, P], F32, name=f"pt{e}") for e in range(E)]
        py = [psum.tile([P, 2, C], F32, name=f"py{e}") for e in range(E)]

        nc.vector.memset(w1s[:].rearrange("p a b -> p (a b)").bitcast(I32), 0)
        nc.vector.memset(w2s[:].rearrange("p a b -> p (a b)").bitcast(I32), 0)
        nc.vector.memset(warm[:], 0.0)
        for s in range(S):
            nc.vector.memset(xs[s][:].bitcast(I32), 0)
        make_identity(nc, ident[:])
        for n in range(2):
            nc.gpsimd.memset(win[n][:], 0.0)

        def load_x(s, a, b):
            nc.sync.dma_start(x[s][:, :, a:b], xT[512 * s : 512 * s + 512, a:b].rearrange("(p j) t -> p j t", j=4))

        def load_w1(e0, e1, s0, s1):
            for e in range(e0, e1):
                nc.sync.dma_start(w1[:, e, s0:s1, :].bitcast(I32), w1_words[e, s0:s1].rearrange("s p b -> p s b").bitcast(I32))

        def load_w1s(e):
            for quad in range(4):
                nc.sync.dma_start(
                    w1s[32 * quad : 32 * quad + 4, e * S : e * S + S, :].bitcast(I32),
                    w1_scales[e, :, 4 * quad : 4 * quad + 4, :].rearrange("s q i -> q s i").bitcast(I32),
                )

        for b in range(0, T, C):
            load_x(0, b, b + C)
        nc.sync.dma_start(offsets[:], offs)
        nc.scalar.activation(warm[:], warm[:], ACT.Gelu_apprx_tanh)
        load_x(1, 0, A)
        load_x(1, A, T)
        load_x(2, 0, A)
        load_x(2, A, T)
        load_w1(0, 1, 0, 2)
        load_x(3, 0, A)
        load_x(3, A, T)
        load_w1s(0)
        load_w1(1, 2, 0, 2)
        load_w1(0, 1, 2, 4)
        load_w1s(1)
        load_w1(1, 2, 2, 4)
        nc.sync.dma_start(w2[:].bitcast(I32), w2_words.rearrange("e s p b -> p (e s) b").bitcast(I32))
        for quad in range(4):
            nc.gpsimd.dma_start(
                w2s[32 * quad : 32 * quad + 4].bitcast(I32),
                w2_scales.rearrange("e s q i -> q (e s) i")[4 * quad : 4 * quad + 4].bitcast(I32),
            )

        def cast(engine, s, a, b):
            dst = xb[s][:, a:b, :]
            src = x[s][:, :, a:b].rearrange("p j t -> p t j")
            if engine == "s":
                nc.scalar.activation(dst, src, ACT.Copy)
            else:
                nc.vector.tensor_copy(dst, src)

        def quant(s, a, b):
            nc.vector.quantize_mx(
                out=xw[s][:, a:b].bitcast(FP8X4),
                scales=xs[s][:, a:b],
                in_=xb[s][:, a:b, :].rearrange("p t j -> p (t j)"),
            )

        def gather_words(s, e0, e1):
            nc.vector.tensor_copy(gw[s][:, e0 * C : e1 * C], xw[s][:].indirect(offsets[:, e0 * C // 16 : e1 * C // 16]))

        def gather_scales(s, e0, e1):
            nc.vector.tensor_copy(gs[s][:, e0 * C : e1 * C], xs[s][:].indirect(offsets[:, e0 * C // 16 : e1 * C // 16]))

        def up(s, m):
            e = m // 2
            cols = slice(P * m, P * m + P)
            nc.tensor.matmul_mx(
                out=pa[m][:],
                lhsT=gw[s][:, cols].bitcast(FP8X4),
                lhsT_scale=gs[s][:, cols],
                rhs=w1[:, e, s, :].bitcast(FP4X4),
                rhs_scale=w1s[:, e * S + s, :],
                start=(s == 0),
                stop=(s == S - 1),
            )

        nc.sync.dma_start(g[:], gate[0:P, :])
        for n in range(2):
            nc.sync.dma_start(res[n][:], xr[P * n : P * n + P, :])

        last = S - 1
        cast("s", 0, 0, 192)
        cast("v", 0, 192, 256)
        quant(0, 0, 256)
        cast("s", 0, 256, 448)
        cast("v", 0, 448, 512)
        quant(0, 256, 512)
        cast("s", 0, 512, 704)
        cast("v", 0, 704, 768)
        quant(0, 512, 768)
        gather_scales(0, 0, E)
        cast("s", 1, 0, 288)
        cast("v", 1, 288, 512)
        cast("s", 1, 512, 544)
        cast("v", 1, 544, 768)
        gather_words(0, 0, 1)
        quant(1, 0, A)
        quant(1, A, T)
        gather_words(0, 1, 2)
        cast("s", 2, 0, 448)
        cast("v", 2, 448, 512)
        cast("s", 2, 512, 736)
        cast("v", 2, 736, 768)
        gather_scales(1, 0, E)
        gather_words(1, 0, 1)
        quant(2, 0, A)
        quant(2, A, T)
        gather_words(1, 1, 2)
        cast("s", 3, 0, 480)
        cast("v", 3, 480, 512)
        gather_scales(2, 0, E)
        cast("s", 3, 512, 672)
        cast("v", 3, 672, 768)
        gather_words(2, 0, 1)
        quant(3, 0, A)
        quant(3, A, T)

        def gelu_turn(m):
            nc.scalar.activation(h[m][:], pa[m][:], ACT.Gelu_apprx_tanh)
            words = h[m][:].bitcast(F32)
            for u in range(2):
                nc.tensor.transpose(pt[m // 2][:, m % 2, u, :], words[:, u : H // 2 : 2], ident[:])

        def lay(m, copy):
            i = m % 2
            copy(
                hg[m // 2][:, H * i : H * i + H].bitcast(F32).rearrange("p (r u) -> p r u", u=2),
                pt[m // 2][:, i].rearrange("p u r -> p r u"),
            )

        def quant_h(m):
            e, cols = m // 2, slice(P * (m % 2), P * (m % 2) + P)
            nc.vector.quantize_mx(out=hw[e][:, cols].bitcast(FP8X4), scales=hs[e][:, cols], in_=hg[e][:, H * (m % 2) : H * (m % 2) + H])

        def down(e):
            for n in range(2):
                nc.tensor.matmul_mx(
                    out=py[e][:, n, :],
                    lhsT=w2[:, e, N * n : N * n + N].bitcast(FP4X4),
                    lhsT_scale=w2s[:, e, P * n : P * n + P],
                    rhs=hw[e][:].bitcast(FP8X4),
                    rhs_scale=hs[e][:],
                    start=True,
                    stop=True,
                )

        def weigh(e, n):
            nc.vector.tensor_tensor(y[e][:, n, :], py[e][:, n, :], g[:, e * C : (e + 1) * C], MULT)

        def scatter(e, n):
            nc.vector.tensor_copy(win[n][:].indirect(offsets[:, e * C // 16 : (e + 1) * C // 16]), y[e][:, n, :])

        up(0, 0)
        up(1, 0)
        up(2, 0)
        up(0, 1)
        up(1, 1)
        up(2, 1)
        gather_scales(3, 0, 1)
        gather_words(3, 0, 1)
        up(3, 0)
        up(3, 1)
        gelu_turn(0)
        gelu_turn(1)
        gather_words(2, 1, 2)
        gather_scales(3, 1, 2)
        gather_words(3, 1, 2)
        lay(0, nc.scalar.copy)
        lay(1, nc.vector.tensor_copy)
        quant_h(0)
        quant_h(1)
        down(0)
        up(0, 2)
        up(1, 2)
        up(2, 2)
        up(0, 3)
        up(1, 3)
        up(2, 3)
        up(3, 2)
        up(3, 3)
        gelu_turn(2)
        gelu_turn(3)
        lay(2, nc.scalar.copy)
        lay(3, nc.scalar.copy)
        weigh(0, 0)
        weigh(0, 1)
        scatter(0, 0)
        quant_h(2)
        quant_h(3)
        down(1)
        scatter(0, 1)
        weigh(1, 0)
        weigh(1, 1)
        scatter(1, 0)
        scatter(1, 1)
        for n in range(2):
            for a, b in ((0, T // 2), (T // 2, T)):
                engine = nc.gpsimd if n == 0 else nc.vector
                engine.tensor_tensor(o[n][:, a:b], win[n][:, a:b], res[n][:, a:b], ADD)
                nc.sync.dma_start(out[P * n : P * n + P, a:b], o[n][:, a:b])
